import numpy as np
import ml_dtypes


def mxq(x, axis, fmt="e4m3"):
    dtype, down = {"e4m3": (ml_dtypes.float8_e4m3fn, 7), "e5m2": (ml_dtypes.float8_e5m2, 14)}[fmt]
    v = np.moveaxis(np.asarray(x, np.float32).astype(ml_dtypes.bfloat16).astype(np.float64), axis, -1)
    blocks = v.reshape(v.shape[:-1] + (-1, 32))
    amax = np.abs(blocks).max(-1, keepdims=True)
    byte = np.maximum(np.where(amax > 0, np.frexp(amax)[1] - 1 + 127, 0) - down, 1)
    scale = np.exp2(byte - 127.0)
    codes = (blocks / scale).astype(np.float32).astype(dtype).astype(np.float64)
    return np.moveaxis((codes * scale).reshape(v.shape), -1, axis)


WIDE = False


def mx_kscale(k):
    if not WIDE:
        return np.ones(k)
    levels = np.array([10, -10, 5, -5, 0])
    if k % 512:
        return np.exp2(np.random.permutation(np.resize(levels, k // 32))).repeat(32)
    a = np.empty((k // 512, 16))
    for p in range(k // 512):
        a[p, :8] = np.random.permutation(np.resize(levels, 8))
        for g in range(8):
            far = levels[np.abs(levels - a[p, g]) >= 10]
            a[p, g + 8] = far[np.random.randint(len(far))]
    return np.exp2(a.ravel()).repeat(32)


def f64(x):
    return np.asarray(x).astype(np.float64)


def striped(idx):
    return np.tile(idx.reshape(-1, 16).T, (8, 1)).astype(np.uint16)


def unstriped(offs):
    return offs[:16].T.reshape(-1).astype(np.int64)


def pack_weight(w):
    k, n = w.shape
    w = f64(np.asarray(w, np.float32).astype(ml_dtypes.bfloat16)).reshape(k // 32, 32, n)
    amax = np.abs(w).max(1)
    byte = np.clip(np.where(amax > 0, np.frexp(amax)[1] - 1 + 127 - 7, 1), 1, 254)
    scaled = (w * np.exp2(127.0 - byte)[:, None, :]).reshape(k, n).astype(np.float32)
    words = np.ascontiguousarray(scaled.reshape(k // 512, 128, 4, n).transpose(0, 1, 3, 2)).astype(ml_dtypes.float8_e4m3fn).view(np.uint8)
    return words, np.ascontiguousarray(byte.astype(np.uint8).reshape(k // 512, 16, n))


def unpack_weight(words, scales):
    g, p, n, _ = words.shape
    vals = np.ascontiguousarray(words).view(ml_dtypes.float8_e4m3fn).astype(np.float64) * np.repeat(np.exp2(scales.astype(np.float64) - 127.0), 8, axis=1)[..., None]
    return vals.transpose(0, 1, 3, 2).reshape(g * 512, n)


K, T, S, N = 512, 4096, 1024, 128


def setup_inputs():
    n = np.random.standard_normal
    s = mx_kscale(K)[:, None]
    packed_xT = pack_weight(n((K, T)) * s)
    return {
        "x_words": packed_xT[0],
        "x_scales": packed_xT[1],
        "w1": (n((K, N)) / np.sqrt(K) / s).astype(np.float32),
        "offs": striped(np.random.permutation(T)[:S]),
    }


def reference(x_words, x_scales, w1, offs):
    xq = unpack_weight(x_words, x_scales)[:, unstriped(offs)]
    y = mxq(f64(w1), 0, "e4m3").T @ xq
    e = np.exp(y - y.max(axis=1, keepdims=True))
    return e / e.sum(axis=1, keepdims=True)

@@ -1,0 +1,112 @@
+from contextlib import ExitStack
+
+import concourse.mybir as mybir
+
+K, T, S, N = 512, 4096, 1024, 128
+FLOPS = 2 * K * S * N
+
+F32 = mybir.dt.float32
+BF16 = mybir.dt.bfloat16
+I32 = mybir.dt.int32
+U32 = mybir.dt.uint32
+U16 = mybir.dt.uint16
+U8 = mybir.dt.uint8
+FP8X4 = mybir.dt.float8_e4m3fn_x4
+ALU = mybir.AluOpType
+EXP = mybir.ActivationFunctionType.Exp
+AX = mybir.AxisListType.X
+
+P = 128
+PACK = 4
+HALF = S // 2
+PIECES = [256,256,256,256]
+CHUNKS = [256,256,256,256]
+SPREAD = True
+
+
+def tile_picked_rank_none_p_kernel(tc, x_words, x_scales, w1, offs, out):
+    nc = tc.nc
+    with ExitStack() as ctx:
+        keep = ctx.enter_context(tc.tile_pool(name="keep", bufs=1))
+        psum = ctx.enter_context(tc.psum_pool(name="psum", bufs=1))
+
+        offsets = keep.tile([P, S // 16], U16, name="offsets")
+        w_raw = keep.tile([P, PACK, N], F32, name="w_raw")
+        words = keep.tile([P, T], U32, name="words", align_bytes=64)
+        scales = keep.tile([P, T], U8, name="scales", tag="turns", align_bytes=64)
+
+        nc.vector.memset(scales[:].bitcast(I32), 0)
+        nc.sync.dma_start(offsets[:], offs)
+        nc.sync.dma_start(out=w_raw[:], in_=w1.rearrange("(p j) n -> p j n", j=PACK))
+        nc.sync.dma_start(out=words[:].bitcast(I32), in_=x_words[0].rearrange("p n t -> p (n t)").bitcast(I32))
+        if SPREAD:
+            nc.scalar.dma_start(out=scales[0:P:8, :].bitcast(I32), in_=x_scales[0].bitcast(I32))
+        else:
+            for q in range(4):
+                nc.scalar.dma_start(out=scales[32 * q : 32 * q + 4, :].bitcast(I32), in_=x_scales[0, 4 * q : 4 * q + 4, :].bitcast(I32))
+
+        warm_in = keep.tile([P, 1], F32, name="warm_in")
+        warm_out = keep.tile([P, 1], F32, name="warm_out")
+        nc.vector.memset(warm_in[:], 0.0)
+        nc.scalar.activation(warm_out[:], warm_in[:], EXP)
+
+        w_bf = keep.tile([P, N, PACK], BF16, name="w_bf", align_bytes=64)
+        w_codes = keep.tile([P, N], U32, name="w_codes", align_bytes=64)
+        w_scales = keep.tile([P, N], U8, name="w_scales", align_bytes=64)
+        nc.vector.tensor_copy(out=w_bf[:], in_=w_raw[:].rearrange("p j n -> p n j"))
+        nc.vector.quantize_mx(out=w_codes[:].bitcast(FP8X4), scales=w_scales[:], in_=w_bf[:].rearrange("p n j -> p (n j)"))
+
+        picked_scales = keep.tile([P, S], U8, name="picked_scales", align_bytes=64)
+        nc.vector.tensor_copy(picked_scales[:], scales[:].indirect(offsets[:]))
+        plane = picked_scales
+        if SPREAD:
+            plane = keep.tile([P, S], U8, name="plane", align_bytes=64)
+            for r in range(4):
+                nc.scalar.dma_start(out=plane[r:P:32, :].bitcast(I32), in_=picked_scales[8 * r : P : 32, :].bitcast(I32))
+
+        picked = keep.tile([P, S], U32, name="picked", tag="turns", align_bytes=64)
+        for h in range(2):
+            nc.vector.tensor_copy(picked[:, h * HALF : (h + 1) * HALF], words[:].indirect(offsets[:, h * HALF // 16 : (h + 1) * HALF // 16]))
+
+        n_p = len(PIECES)
+        neg_max = keep.tile([P, n_p], F32, name="neg_max")
+        sums = keep.tile([P, n_p], F32, name="sums")
+        exps = []
+        c0 = 0
+        for i, width in enumerate(PIECES):
+            acc = psum.tile([P, width], F32, name=f"acc{i}")
+            nc.tensor.matmul_mx(
+                out=acc[:],
+                lhsT=w_codes[:].bitcast(FP8X4),
+                lhsT_scale=w_scales[:],
+                rhs=picked[:, c0 : c0 + width].bitcast(FP8X4),
+                rhs_scale=plane[:, c0 : c0 + width],
+                start=True,
+                stop=True,
+            )
+            nc.vector.tensor_reduce(neg_max[:, i : i + 1], acc[:], AX, ALU.max, negate=True)
+            e = keep.tile([P, width], F32, name=f"e{i}")
+            nc.scalar.activation(e[:], acc[:], EXP, bias=neg_max[:, i : i + 1], accum_out=sums[:, i : i + 1])
+            exps.append((c0, width, e))
+            c0 = c0 + width
+
+        neg_top = keep.tile([P, 1], F32, name="neg_top")
+        nc.vector.tensor_reduce(neg_top[:], neg_max[:], AX, ALU.min)
+        adjust = keep.tile([P, n_p], F32, name="adjust")
+        nc.scalar.activation(adjust[:], neg_max[:], EXP, bias=neg_top[:], scale=-1.0)
+        terms = keep.tile([P, n_p], F32, name="terms")
+        total = keep.tile([P, 1], F32, name="total")
+        nc.vector.scalar_tensor_tensor(terms[:], sums[:], 1.0, adjust[:], ALU.mult, ALU.mult, accum_out=total[:])
+        recip = keep.tile([P, 1], F32, name="recip")
+        nc.vector.reciprocal(recip[:], total[:])
+
+        c0 = 0
+        for j, width in enumerate(CHUNKS):
+            res = keep.tile([P, width], F32, name=f"res{j}")
+            for i, (p0, pw, e) in enumerate(exps):
+                a, b = max(p0, c0), min(p0 + pw, c0 + width)
+                if a < b:
+                    nc.vector.tensor_scalar(res[:, a - c0 : b - c0], e[:, a - p0 : b - p0], adjust[:, i : i + 1], recip[:], ALU.mult, ALU.mult)
+            queue = nc.sync if j % 2 == 0 else nc.scalar
+            queue.dma_start(out=out[:, c0 : c0 + width], in_=res[:])
+            c0 = c0 + width

@@ -20,7 +20,7 @@ P = 128
 PACK = 4
 HALF = S // 2
 PIECES = [256,256,256,256]
-CHUNKS = [256,256,256,256]
+CHUNKS = [256,256,512]
 SPREAD = True
 
 
@@ -35,12 +35,13 @@ def tile_picked_rank_none_p_kernel(tc, x_words, x_scales, w1, offs, out):
         words = keep.tile([P, T], U32, name="words", align_bytes=64)
         scales = keep.tile([P, T], U8, name="scales", tag="turns", align_bytes=64)
 
-        nc.vector.memset(scales[:].bitcast(I32), 0)
+        nc.vector.memset(scales[0:112, :].bitcast(I32), 0)
+        nc.sync.dma_start(out=scales[112:P, :].bitcast(I32), in_=x_scales[0].bitcast(I32))
         nc.sync.dma_start(offsets[:], offs)
         nc.sync.dma_start(out=w_raw[:], in_=w1.rearrange("(p j) n -> p j n", j=PACK))
         nc.sync.dma_start(out=words[:].bitcast(I32), in_=x_words[0].rearrange("p n t -> p (n t)").bitcast(I32))
         if SPREAD:
-            nc.scalar.dma_start(out=scales[0:P:8, :].bitcast(I32), in_=x_scales[0].bitcast(I32))
+            pass
         else:
             for q in range(4):
                 nc.scalar.dma_start(out=scales[32 * q : 32 * q + 4, :].bitcast(I32), in_=x_scales[0, 4 * q : 4 * q + 4, :].bitcast(I32))
@@ -62,7 +63,7 @@ def tile_picked_rank_none_p_kernel(tc, x_words, x_scales, w1, offs, out):
         if SPREAD:
             plane = keep.tile([P, S], U8, name="plane", align_bytes=64)
             for r in range(4):
-                nc.scalar.dma_start(out=plane[r:P:32, :].bitcast(I32), in_=picked_scales[8 * r : P : 32, :].bitcast(I32))
+                nc.scalar.dma_start(out=plane[r:P:32, :].bitcast(I32), in_=picked_scales[112 + r : P : 4, :].bitcast(I32))
 
         picked = keep.tile([P, S], U32, name="picked", tag="turns", align_bytes=64)
         for h in range(2):

@@ -21,7 +21,6 @@ PACK = 4
 HALF = S // 2
 PIECES = [256,256,256,256]
 CHUNKS = [256,256,512]
-SPREAD = True
 
 
 def tile_picked_rank_none_p_kernel(tc, x_words, x_scales, w1, offs, out):
@@ -35,16 +34,13 @@ def tile_picked_rank_none_p_kernel(tc, x_words, x_scales, w1, offs, out):
         words = keep.tile([P, T], U32, name="words", align_bytes=64)
         scales = keep.tile([P, T], U8, name="scales", tag="turns", align_bytes=64)
 
-        nc.vector.memset(scales[0:112, :].bitcast(I32), 0)
-        nc.sync.dma_start(out=scales[112:P, :].bitcast(I32), in_=x_scales[0].bitcast(I32))
-        nc.sync.dma_start(offsets[:], offs)
+        nc.vector.memset(scales[:].bitcast(I32), 0)
+        x_rows = x_words[0].rearrange("p n t -> p (n t)").bitcast(I32)
         nc.sync.dma_start(out=w_raw[:], in_=w1.rearrange("(p j) n -> p j n", j=PACK))
-        nc.sync.dma_start(out=words[:].bitcast(I32), in_=x_words[0].rearrange("p n t -> p (n t)").bitcast(I32))
-        if SPREAD:
-            pass
-        else:
-            for q in range(4):
-                nc.scalar.dma_start(out=scales[32 * q : 32 * q + 4, :].bitcast(I32), in_=x_scales[0, 4 * q : 4 * q + 4, :].bitcast(I32))
+        nc.sync.dma_start(offsets[:], offs)
+        nc.sync.dma_start(out=words[:, 0:1024].bitcast(I32), in_=x_rows[:, 0:1024])
+        nc.sync.dma_start(out=scales[32:96:4, :].bitcast(I32), in_=x_scales[0].bitcast(I32))
+        nc.sync.dma_start(out=words[:, 1024:T].bitcast(I32), in_=x_rows[:, 1024:T])
 
         warm_in = keep.tile([P, 1], F32, name="warm_in")
         warm_out = keep.tile([P, 1], F32, name="warm_out")
@@ -59,11 +55,9 @@ def tile_picked_rank_none_p_kernel(tc, x_words, x_scales, w1, offs, out):
 
         picked_scales = keep.tile([P, S], U8, name="picked_scales", align_bytes=64)
         nc.vector.tensor_copy(picked_scales[:], scales[:].indirect(offsets[:]))
-        plane = picked_scales
-        if SPREAD:
-            plane = keep.tile([P, S], U8, name="plane", align_bytes=64)
-            for r in range(4):
-                nc.scalar.dma_start(out=plane[r:P:32, :].bitcast(I32), in_=picked_scales[112 + r : P : 4, :].bitcast(I32))
+        plane = keep.tile([P, S], U8, name="plane", align_bytes=64)
+        for r in range(4):
+            nc.scalar.dma_start(out=plane[r:P:32, :].bitcast(I32), in_=picked_scales[32 + 4 * r : 96 : 16, :].bitcast(I32))
 
         picked = keep.tile([P, S], U32, name="picked", tag="turns", align_bytes=64)
         for h in range(2):

@@ -42,22 +42,20 @@ def tile_picked_rank_none_p_kernel(tc, x_words, x_scales, w1, offs, out):
         nc.sync.dma_start(out=scales[32:96:4, :].bitcast(I32), in_=x_scales[0].bitcast(I32))
         nc.sync.dma_start(out=words[:, 1024:T].bitcast(I32), in_=x_rows[:, 1024:T])
 
-        warm_in = keep.tile([P, 1], F32, name="warm_in")
-        warm_out = keep.tile([P, 1], F32, name="warm_out")
-        nc.vector.memset(warm_in[:], 0.0)
-        nc.scalar.activation(warm_out[:], warm_in[:], EXP)
-
         w_bf = keep.tile([P, N, PACK], BF16, name="w_bf", align_bytes=64)
         w_codes = keep.tile([P, N], U32, name="w_codes", align_bytes=64)
         w_scales = keep.tile([P, N], U8, name="w_scales", align_bytes=64)
         nc.vector.tensor_copy(out=w_bf[:], in_=w_raw[:].rearrange("p j n -> p n j"))
         nc.vector.quantize_mx(out=w_codes[:].bitcast(FP8X4), scales=w_scales[:], in_=w_bf[:].rearrange("p n j -> p (n j)"))
 
-        picked_scales = keep.tile([P, S], U8, name="picked_scales", align_bytes=64)
-        nc.vector.tensor_copy(picked_scales[:], scales[:].indirect(offsets[:]))
-        plane = keep.tile([P, S], U8, name="plane", align_bytes=64)
-        for r in range(4):
-            nc.scalar.dma_start(out=plane[r:P:32, :].bitcast(I32), in_=picked_scales[32 + 4 * r : 96 : 16, :].bitcast(I32))
+        planes = []
+        for h in range(2):
+            picked_scales = keep.tile([P, HALF], U8, name=f"picked_scales{h}", align_bytes=64)
+            nc.vector.tensor_copy(picked_scales[:], scales[:].indirect(offsets[:, h * HALF // 16 : (h + 1) * HALF // 16]))
+            plane = keep.tile([P, HALF], U8, name=f"plane{h}", align_bytes=64)
+            for r in range(4):
+                (nc.scalar, nc.sync)[h].dma_start(out=plane[r:P:32, :].bitcast(I32), in_=picked_scales[32 + 4 * r : 96 : 16, :].bitcast(I32))
+            planes.append(plane)
 
         picked = keep.tile([P, S], U32, name="picked", tag="turns", align_bytes=64)
         for h in range(2):
@@ -75,7 +73,7 @@ def tile_picked_rank_none_p_kernel(tc, x_words, x_scales, w1, offs, out):
                 lhsT=w_codes[:].bitcast(FP8X4),
                 lhsT_scale=w_scales[:],
                 rhs=picked[:, c0 : c0 + width].bitcast(FP8X4),
-                rhs_scale=plane[:, c0 : c0 + width],
+                rhs_scale=planes[c0 // HALF][:, c0 % HALF : c0 % HALF + width],
                 start=True,
                 stop=True,
             )

@@ -14,12 +14,14 @@ U8 = mybir.dt.uint8
 FP8X4 = mybir.dt.float8_e4m3fn_x4
 ALU = mybir.AluOpType
 EXP = mybir.ActivationFunctionType.Exp
+COPY = mybir.ActivationFunctionType.Copy
 AX = mybir.AxisListType.X
 
 P = 128
 PACK = 4
 HALF = S // 2
-PIECES = [256,256,256,256]
+PIECES = [256,256,128,128,128,128]
+CAP = 2.0**100
 CHUNKS = [256,256,512]
 
 
@@ -30,23 +32,22 @@ def tile_picked_rank_none_p_kernel(tc, x_words, x_scales, w1, offs, out):
         psum = ctx.enter_context(tc.psum_pool(name="psum", bufs=1))
 
         offsets = keep.tile([P, S // 16], U16, name="offsets")
-        w_raw = keep.tile([P, PACK, N], F32, name="w_raw")
+        w_raw = keep.tile([P, PACK, N], F32, name="w_raw", tag="late", align_bytes=64)
         words = keep.tile([P, T], U32, name="words", align_bytes=64)
         scales = keep.tile([P, T], U8, name="scales", tag="turns", align_bytes=64)
 
-        nc.vector.memset(scales[:].bitcast(I32), 0)
+        nc.vector.memset(scales[:, 0:2560].bitcast(I32), 0)
+        nc.gpsimd.memset(scales[:, 2560:T].bitcast(I32), 0)
         x_rows = x_words[0].rearrange("p n t -> p (n t)").bitcast(I32)
-        nc.sync.dma_start(out=w_raw[:], in_=w1.rearrange("(p j) n -> p j n", j=PACK))
         nc.sync.dma_start(offsets[:], offs)
         nc.sync.dma_start(out=words[:, 0:1024].bitcast(I32), in_=x_rows[:, 0:1024])
         nc.sync.dma_start(out=scales[32:96:4, :].bitcast(I32), in_=x_scales[0].bitcast(I32))
         nc.sync.dma_start(out=words[:, 1024:T].bitcast(I32), in_=x_rows[:, 1024:T])
+        nc.sync.dma_start(out=w_raw[:], in_=w1.rearrange("(p j) n -> p j n", j=PACK))
 
         w_bf = keep.tile([P, N, PACK], BF16, name="w_bf", align_bytes=64)
         w_codes = keep.tile([P, N], U32, name="w_codes", align_bytes=64)
         w_scales = keep.tile([P, N], U8, name="w_scales", align_bytes=64)
-        nc.vector.tensor_copy(out=w_bf[:], in_=w_raw[:].rearrange("p j n -> p n j"))
-        nc.vector.quantize_mx(out=w_codes[:].bitcast(FP8X4), scales=w_scales[:], in_=w_bf[:].rearrange("p n j -> p (n j)"))
 
         planes = []
         for h in range(2):
@@ -54,12 +55,15 @@ def tile_picked_rank_none_p_kernel(tc, x_words, x_scales, w1, offs, out):
             nc.vector.tensor_copy(picked_scales[:], scales[:].indirect(offsets[:, h * HALF // 16 : (h + 1) * HALF // 16]))
             plane = keep.tile([P, HALF], U8, name=f"plane{h}", align_bytes=64)
             for r in range(4):
-                (nc.scalar, nc.sync)[h].dma_start(out=plane[r:P:32, :].bitcast(I32), in_=picked_scales[32 + 4 * r : 96 : 16, :].bitcast(I32))
+                nc.sync.dma_start(out=plane[r:P:32, :].bitcast(I32), in_=picked_scales[32 + 4 * r : 96 : 16, :].bitcast(I32))
             planes.append(plane)
 
-        picked = keep.tile([P, S], U32, name="picked", tag="turns", align_bytes=64)
-        for h in range(2):
-            nc.vector.tensor_copy(picked[:, h * HALF : (h + 1) * HALF], words[:].indirect(offsets[:, h * HALF // 16 : (h + 1) * HALF // 16]))
+        picked = [keep.tile([P, HALF], U32, name="picked0", tag="turns", align_bytes=64)]
+        nc.vector.tensor_copy(picked[0][:], words[:].indirect(offsets[:, 0 : HALF // 16]))
+        nc.scalar.activation(w_bf[:].rearrange("p (c i) j -> p c j i", i=4), w_raw[:].rearrange("p j (c i) -> p c j i", i=4), COPY)
+        nc.vector.quantize_mx(out=w_codes[:].bitcast(FP8X4), scales=w_scales[:], in_=w_bf[:].rearrange("p n j -> p (n j)"))
+        picked.append(keep.tile([P, HALF], U32, name="picked1", tag="late", align_bytes=64))
+        nc.vector.tensor_copy(picked[1][:], words[:].indirect(offsets[:, HALF // 16 : S // 16]))
 
         n_p = len(PIECES)
         neg_max = keep.tile([P, n_p], F32, name="neg_max")
@@ -72,7 +76,7 @@ def tile_picked_rank_none_p_kernel(tc, x_words, x_scales, w1, offs, out):
                 out=acc[:],
                 lhsT=w_codes[:].bitcast(FP8X4),
                 lhsT_scale=w_scales[:],
-                rhs=picked[:, c0 : c0 + width].bitcast(FP8X4),
+                rhs=picked[c0 // HALF][:, c0 % HALF : c0 % HALF + width].bitcast(FP8X4),
                 rhs_scale=planes[c0 // HALF][:, c0 % HALF : c0 % HALF + width],
                 start=True,
                 stop=True,
@@ -84,12 +88,14 @@ def tile_picked_rank_none_p_kernel(tc, x_words, x_scales, w1, offs, out):
             c0 = c0 + width
 
         neg_top = keep.tile([P, 1], F32, name="neg_top")
-        nc.vector.tensor_reduce(neg_top[:], neg_max[:], AX, ALU.min)
+        nc.vector.tensor_reduce(neg_top[:], neg_max[:, 0 : n_p - 1], AX, ALU.min)
         adjust = keep.tile([P, n_p], F32, name="adjust")
         nc.scalar.activation(adjust[:], neg_max[:], EXP, bias=neg_top[:], scale=-1.0)
         terms = keep.tile([P, n_p], F32, name="terms")
         total = keep.tile([P, 1], F32, name="total")
-        nc.vector.scalar_tensor_tensor(terms[:], sums[:], 1.0, adjust[:], ALU.mult, ALU.mult, accum_out=total[:])
+        nc.vector.scalar_tensor_tensor(terms[:], adjust[:], CAP, sums[:], ALU.min, ALU.mult, accum_out=total[:])
+        capped = keep.tile([P, n_p], F32, name="capped")
+        nc.vector.tensor_scalar(capped[:], adjust[:], CAP, None, ALU.min)
         recip = keep.tile([P, 1], F32, name="recip")
         nc.vector.reciprocal(recip[:], total[:])
 
@@ -99,7 +105,7 @@ def tile_picked_rank_none_p_kernel(tc, x_words, x_scales, w1, offs, out):
             for i, (p0, pw, e) in enumerate(exps):
                 a, b = max(p0, c0), min(p0 + pw, c0 + width)
                 if a < b:
-                    nc.vector.tensor_scalar(res[:, a - c0 : b - c0], e[:, a - p0 : b - p0], adjust[:, i : i + 1], recip[:], ALU.mult, ALU.mult)
+                    nc.vector.tensor_scalar(res[:, a - c0 : b - c0], e[:, a - p0 : b - p0], capped[:, i : i + 1], recip[:], ALU.mult, ALU.mult)
             queue = nc.sync if j % 2 == 0 else nc.scalar
             queue.dma_start(out=out[:, c0 : c0 + width], in_=res[:])
             c0 = c0 + width

@@ -22,7 +22,7 @@ PACK = 4
 HALF = S // 2
 PIECES = [256,256,128,128,128,128]
 CAP = 2.0**100
-CHUNKS = [256,256,512]
+CHUNKS = [256,256,256,256]
 
 
 def tile_picked_rank_none_p_kernel(tc, x_words, x_scales, w1, offs, out):
@@ -32,35 +32,37 @@ def tile_picked_rank_none_p_kernel(tc, x_words, x_scales, w1, offs, out):
         psum = ctx.enter_context(tc.psum_pool(name="psum", bufs=1))
 
         offsets = keep.tile([P, S // 16], U16, name="offsets")
-        w_raw = keep.tile([P, PACK, N], F32, name="w_raw", tag="late", align_bytes=64)
+        w_raw = keep.tile([P, PACK - 1, N], F32, name="w_raw", tag="late", align_bytes=64)
+        w_first = keep.tile([P, N], F32, name="w_first")
         words = keep.tile([P, T], U32, name="words", align_bytes=64)
         scales = keep.tile([P, T], U8, name="scales", tag="turns", align_bytes=64)
 
         nc.vector.memset(scales[:, 0:2560].bitcast(I32), 0)
         nc.gpsimd.memset(scales[:, 2560:T].bitcast(I32), 0)
         x_rows = x_words[0].rearrange("p n t -> p (n t)").bitcast(I32)
-        nc.sync.dma_start(offsets[:], offs)
+        w_rows = w1.rearrange("(p j) n -> p j n", j=PACK)
         nc.sync.dma_start(out=words[:, 0:1024].bitcast(I32), in_=x_rows[:, 0:1024])
+        nc.sync.dma_start(offsets[:], offs)
+        nc.sync.dma_start(out=w_first[:], in_=w_rows[:, 0, :])
         nc.sync.dma_start(out=scales[32:96:4, :].bitcast(I32), in_=x_scales[0].bitcast(I32))
-        nc.sync.dma_start(out=words[:, 1024:T].bitcast(I32), in_=x_rows[:, 1024:T])
-        nc.sync.dma_start(out=w_raw[:], in_=w1.rearrange("(p j) n -> p j n", j=PACK))
+        for c in range(1024, T, 1024):
+            nc.sync.dma_start(out=words[:, c : c + 1024].bitcast(I32), in_=x_rows[:, c : c + 1024])
+        nc.sync.dma_start(out=w_raw[:], in_=w_rows[:, 1:PACK, :])
 
         w_bf = keep.tile([P, N, PACK], BF16, name="w_bf", align_bytes=64)
         w_codes = keep.tile([P, N], U32, name="w_codes", align_bytes=64)
         w_scales = keep.tile([P, N], U8, name="w_scales", align_bytes=64)
 
-        planes = []
-        for h in range(2):
-            picked_scales = keep.tile([P, HALF], U8, name=f"picked_scales{h}", align_bytes=64)
-            nc.vector.tensor_copy(picked_scales[:], scales[:].indirect(offsets[:, h * HALF // 16 : (h + 1) * HALF // 16]))
-            plane = keep.tile([P, HALF], U8, name=f"plane{h}", align_bytes=64)
-            for r in range(4):
-                nc.sync.dma_start(out=plane[r:P:32, :].bitcast(I32), in_=picked_scales[32 + 4 * r : 96 : 16, :].bitcast(I32))
-            planes.append(plane)
+        picked_scales = keep.tile([P, S], U8, name="picked_scales", align_bytes=64)
+        nc.vector.tensor_copy(picked_scales[:], scales[:].indirect(offsets[:]))
+        plane = keep.tile([P, S], U8, name="plane", align_bytes=64)
+        for r in range(4):
+            nc.sync.dma_start(out=plane[r:P:32, :].bitcast(I32), in_=picked_scales[32 + 4 * r : 96 : 16, :].bitcast(I32))
 
         picked = [keep.tile([P, HALF], U32, name="picked0", tag="turns", align_bytes=64)]
         nc.vector.tensor_copy(picked[0][:], words[:].indirect(offsets[:, 0 : HALF // 16]))
-        nc.scalar.activation(w_bf[:].rearrange("p (c i) j -> p c j i", i=4), w_raw[:].rearrange("p j (c i) -> p c j i", i=4), COPY)
+        nc.scalar.activation(w_bf[:, :, 0], w_first[:], COPY)
+        nc.scalar.activation(w_bf[:, :, 1:PACK].rearrange("p (c i) j -> p c j i", i=4), w_raw[:].rearrange("p j (c i) -> p c j i", i=4), COPY)
         nc.vector.quantize_mx(out=w_codes[:].bitcast(FP8X4), scales=w_scales[:], in_=w_bf[:].rearrange("p n j -> p (n j)"))
         picked.append(keep.tile([P, HALF], U32, name="picked1", tag="late", align_bytes=64))
         nc.vector.tensor_copy(picked[1][:], words[:].indirect(offsets[:, HALF // 16 : S // 16]))
@@ -77,7 +79,7 @@ def tile_picked_rank_none_p_kernel(tc, x_words, x_scales, w1, offs, out):
                 lhsT=w_codes[:].bitcast(FP8X4),
                 lhsT_scale=w_scales[:],
                 rhs=picked[c0 // HALF][:, c0 % HALF : c0 % HALF + width].bitcast(FP8X4),
-                rhs_scale=planes[c0 // HALF][:, c0 % HALF : c0 % HALF + width],
+                rhs_scale=plane[:, c0 : c0 + width],
                 start=True,
                 stop=True,
             )

@@ -22,7 +22,6 @@ PACK = 4
 HALF = S // 2
 PIECES = [256,256,128,128,128,128]
 CAP = 2.0**100
-CHUNKS = [256,256,256,256]
 
 
 def tile_picked_rank_none_p_kernel(tc, x_words, x_scales, w1, offs, out):
@@ -45,19 +44,21 @@ def tile_picked_rank_none_p_kernel(tc, x_words, x_scales, w1, offs, out):
         nc.sync.dma_start(offsets[:], offs)
         nc.sync.dma_start(out=w_first[:], in_=w_rows[:, 0, :])
         nc.sync.dma_start(out=scales[32:96:4, :].bitcast(I32), in_=x_scales[0].bitcast(I32))
-        for c in range(1024, T, 1024):
-            nc.sync.dma_start(out=words[:, c : c + 1024].bitcast(I32), in_=x_rows[:, c : c + 1024])
+        nc.sync.dma_start(out=words[:, 1024:T].bitcast(I32), in_=x_rows[:, 1024:T])
         nc.sync.dma_start(out=w_raw[:], in_=w_rows[:, 1:PACK, :])
 
         w_bf = keep.tile([P, N, PACK], BF16, name="w_bf", align_bytes=64)
         w_codes = keep.tile([P, N], U32, name="w_codes", align_bytes=64)
         w_scales = keep.tile([P, N], U8, name="w_scales", align_bytes=64)
 
-        picked_scales = keep.tile([P, S], U8, name="picked_scales", align_bytes=64)
-        nc.vector.tensor_copy(picked_scales[:], scales[:].indirect(offsets[:]))
-        plane = keep.tile([P, S], U8, name="plane", align_bytes=64)
-        for r in range(4):
-            nc.sync.dma_start(out=plane[r:P:32, :].bitcast(I32), in_=picked_scales[32 + 4 * r : 96 : 16, :].bitcast(I32))
+        planes = []
+        for h in range(2):
+            picked_scales = keep.tile([P, HALF], U8, name=f"picked_scales{h}", align_bytes=64)
+            nc.vector.tensor_copy(picked_scales[:], scales[:].indirect(offsets[:, h * HALF // 16 : (h + 1) * HALF // 16]))
+            plane = keep.tile([P, HALF], U8, name=f"plane{h}", align_bytes=64)
+            for r in range(4):
+                nc.sync.dma_start(out=plane[r:P:32, :].bitcast(I32), in_=picked_scales[32 + 4 * r : 96 : 16, :].bitcast(I32))
+            planes.append(plane)
 
         picked = [keep.tile([P, HALF], U32, name="picked0", tag="turns", align_bytes=64)]
         nc.vector.tensor_copy(picked[0][:], words[:].indirect(offsets[:, 0 : HALF // 16]))
@@ -79,7 +80,7 @@ def tile_picked_rank_none_p_kernel(tc, x_words, x_scales, w1, offs, out):
                 lhsT=w_codes[:].bitcast(FP8X4),
                 lhsT_scale=w_scales[:],
                 rhs=picked[c0 // HALF][:, c0 % HALF : c0 % HALF + width].bitcast(FP8X4),
-                rhs_scale=plane[:, c0 : c0 + width],
+                rhs_scale=planes[c0 // HALF][:, c0 % HALF : c0 % HALF + width],
                 start=True,
                 stop=True,
             )
@@ -101,13 +102,16 @@ def tile_picked_rank_none_p_kernel(tc, x_words, x_scales, w1, offs, out):
         recip = keep.tile([P, 1], F32, name="recip")
         nc.vector.reciprocal(recip[:], total[:])
 
-        c0 = 0
-        for j, width in enumerate(CHUNKS):
-            res = keep.tile([P, width], F32, name=f"res{j}")
-            for i, (p0, pw, e) in enumerate(exps):
-                a, b = max(p0, c0), min(p0 + pw, c0 + width)
-                if a < b:
-                    nc.vector.tensor_scalar(res[:, a - c0 : b - c0], e[:, a - p0 : b - p0], capped[:, i : i + 1], recip[:], ALU.mult, ALU.mult)
-            queue = nc.sync if j % 2 == 0 else nc.scalar
-            queue.dma_start(out=out[:, c0 : c0 + width], in_=res[:])
-            c0 = c0 + width
+        pre = keep.tile([P, 256], F32, name="pre")
+        for i in (2, 3):
+            p0, pw, e = exps[i]
+            nc.scalar.activation(pre[:, p0 - HALF : p0 - HALF + pw], e[:], COPY, scale=adjust[:, i : i + 1])
+        head = keep.tile([P, 256], F32, name="head")
+        rest = keep.tile([P, 768], F32, name="rest")
+        nc.vector.tensor_scalar(head[:], exps[0][2][:], capped[:, 0:1], recip[:], ALU.mult, ALU.mult)
+        nc.sync.dma_start(out=out[:, 0:256], in_=head[:])
+        nc.scalar.activation(rest[:, 256:512], pre[:], COPY, scale=recip[:])
+        for i in (1, 4, 5):
+            p0, pw, e = exps[i]
+            nc.vector.tensor_scalar(rest[:, p0 - 256 : p0 - 256 + pw], e[:], capped[:, i : i + 1], recip[:], ALU.mult, ALU.mult)
+        nc.scalar.dma_start(out=out[:, 256:S], in_=rest[:])

@@ -42,9 +42,9 @@ def tile_picked_rank_none_p_kernel(tc, x_words, x_scales, w1, offs, out):
         w_rows = w1.rearrange("(p j) n -> p j n", j=PACK)
         nc.sync.dma_start(out=words[:, 0:1024].bitcast(I32), in_=x_rows[:, 0:1024])
         nc.sync.dma_start(offsets[:], offs)
-        nc.sync.dma_start(out=w_first[:], in_=w_rows[:, 0, :])
         nc.sync.dma_start(out=scales[32:96:4, :].bitcast(I32), in_=x_scales[0].bitcast(I32))
         nc.sync.dma_start(out=words[:, 1024:T].bitcast(I32), in_=x_rows[:, 1024:T])
+        nc.sync.dma_start(out=w_first[:], in_=w_rows[:, 0, :])
         nc.sync.dma_start(out=w_raw[:], in_=w_rows[:, 1:PACK, :])
 
         w_bf = keep.tile([P, N, PACK], BF16, name="w_bf", align_bytes=64)
@@ -114,4 +114,4 @@ def tile_picked_rank_none_p_kernel(tc, x_words, x_scales, w1, offs, out):
         for i in (1, 4, 5):
             p0, pw, e = exps[i]
             nc.vector.tensor_scalar(rest[:, p0 - 256 : p0 - 256 + pw], e[:], capped[:, i : i + 1], recip[:], ALU.mult, ALU.mult)
-        nc.scalar.dma_start(out=out[:, 256:S], in_=rest[:])
+        nc.sync.dma_start(out=out[:, 256:S], in_=rest[:])

@@ -31,8 +31,8 @@ def tile_picked_rank_none_p_kernel(tc, x_words, x_scales, w1, offs, out):
         psum = ctx.enter_context(tc.psum_pool(name="psum", bufs=1))
 
         offsets = keep.tile([P, S // 16], U16, name="offsets")
-        w_raw = keep.tile([P, PACK - 1, N], F32, name="w_raw", tag="late", align_bytes=64)
-        w_first = keep.tile([P, N], F32, name="w_first")
+        w_raw = keep.tile([P, 2, N], F32, name="w_raw", tag="late", align_bytes=64)
+        w_first = keep.tile([P, 2, N], F32, name="w_first")
         words = keep.tile([P, T], U32, name="words", align_bytes=64)
         scales = keep.tile([P, T], U8, name="scales", tag="turns", align_bytes=64)
 
@@ -44,8 +44,8 @@ def tile_picked_rank_none_p_kernel(tc, x_words, x_scales, w1, offs, out):
         nc.sync.dma_start(offsets[:], offs)
         nc.sync.dma_start(out=scales[32:96:4, :].bitcast(I32), in_=x_scales[0].bitcast(I32))
         nc.sync.dma_start(out=words[:, 1024:T].bitcast(I32), in_=x_rows[:, 1024:T])
-        nc.sync.dma_start(out=w_first[:], in_=w_rows[:, 0, :])
-        nc.sync.dma_start(out=w_raw[:], in_=w_rows[:, 1:PACK, :])
+        nc.sync.dma_start(out=w_first[:], in_=w_rows[:, 0:2, :])
+        nc.sync.dma_start(out=w_raw[:], in_=w_rows[:, 2:PACK, :])
 
         w_bf = keep.tile([P, N, PACK], BF16, name="w_bf", align_bytes=64)
         w_codes = keep.tile([P, N], U32, name="w_codes", align_bytes=64)
@@ -62,9 +62,11 @@ def tile_picked_rank_none_p_kernel(tc, x_words, x_scales, w1, offs, out):
 
         picked = [keep.tile([P, HALF], U32, name="picked0", tag="turns", align_bytes=64)]
         nc.vector.tensor_copy(picked[0][:], words[:].indirect(offsets[:, 0 : HALF // 16]))
-        nc.scalar.activation(w_bf[:, :, 0], w_first[:], COPY)
-        nc.scalar.activation(w_bf[:, :, 1:PACK].rearrange("p (c i) j -> p c j i", i=4), w_raw[:].rearrange("p j (c i) -> p c j i", i=4), COPY)
-        nc.vector.quantize_mx(out=w_codes[:].bitcast(FP8X4), scales=w_scales[:], in_=w_bf[:].rearrange("p n j -> p (n j)"))
+        nc.scalar.activation(w_bf[:, :, 0:2].rearrange("p (c i) j -> p c j i", i=4), w_first[:].rearrange("p j (c i) -> p c j i", i=4), COPY)
+        for a in (0, N // 2):
+            b = a + N // 2
+            nc.scalar.activation(w_bf[:, a:b, 2:PACK].rearrange("p (c i) j -> p c j i", i=4), w_raw[:, :, a:b].rearrange("p j (c i) -> p c j i", i=4), COPY)
+            nc.vector.quantize_mx(out=w_codes[:, a:b].bitcast(FP8X4), scales=w_scales[:, a:b], in_=w_bf[:, a:b, :].rearrange("p n j -> p (n j)"))
         picked.append(keep.tile([P, HALF], U32, name="picked1", tag="late", align_bytes=64))
         nc.vector.tensor_copy(picked[1][:], words[:].indirect(offsets[:, HALF // 16 : S // 16]))
 

@@ -36,8 +36,7 @@ def tile_picked_rank_none_p_kernel(tc, x_words, x_scales, w1, offs, out):
         words = keep.tile([P, T], U32, name="words", align_bytes=64)
         scales = keep.tile([P, T], U8, name="scales", tag="turns", align_bytes=64)
 
-        nc.vector.memset(scales[:, 0:2560].bitcast(I32), 0)
-        nc.gpsimd.memset(scales[:, 2560:T].bitcast(I32), 0)
+        nc.vector.memset(scales[:].bitcast(I32), 0)
         x_rows = x_words[0].rearrange("p n t -> p (n t)").bitcast(I32)
         w_rows = w1.rearrange("(p j) n -> p j n", j=PACK)
         nc.sync.dma_start(out=words[:, 0:1024].bitcast(I32), in_=x_rows[:, 0:1024])

@@ -19,9 +19,13 @@ AX = mybir.AxisListType.X
 
 P = 128
 PACK = 4
+AHEAD = 1024
 HALF = S // 2
-PIECES = [256,256,128,128,128,128]
-CAP = 2.0**100
+GATHERS = [512,256,256]
+PIECES = [[256,128],[128,256],[256]]
+EARLY = 0
+HEAD = 256
+TINY = 2.0**-40
 
 
 def tile_picked_rank_none_p_kernel(tc, x_words, x_scales, w1, offs, out):
@@ -31,24 +35,27 @@ def tile_picked_rank_none_p_kernel(tc, x_words, x_scales, w1, offs, out):
         psum = ctx.enter_context(tc.psum_pool(name="psum", bufs=1))
 
         offsets = keep.tile([P, S // 16], U16, name="offsets")
-        w_raw = keep.tile([P, 2, N], F32, name="w_raw", tag="late", align_bytes=64)
-        w_first = keep.tile([P, 2, N], F32, name="w_first")
         words = keep.tile([P, T], U32, name="words", align_bytes=64)
-        scales = keep.tile([P, T], U8, name="scales", tag="turns", align_bytes=64)
+        scales = keep.tile([P, T], U8, name="scales", align_bytes=64)
+        w_first = keep.tile([P, 2, N], F32, name="w_first")
+        w_bf = keep.tile([P, N, PACK], BF16, name="w_bf", tag="after_second", align_bytes=64)
+        w_second = keep.tile([P, 2, N], F32, name="w_second", tag="after_cast", align_bytes=64)
 
         nc.vector.memset(scales[:].bitcast(I32), 0)
         x_rows = x_words[0].rearrange("p n t -> p (n t)").bitcast(I32)
         w_rows = w1.rearrange("(p j) n -> p j n", j=PACK)
-        nc.sync.dma_start(out=words[:, 0:1024].bitcast(I32), in_=x_rows[:, 0:1024])
+        nc.sync.dma_start(out=words[:, 0:AHEAD].bitcast(I32), in_=x_rows[:, 0:AHEAD])
         nc.sync.dma_start(offsets[:], offs)
         nc.sync.dma_start(out=scales[32:96:4, :].bitcast(I32), in_=x_scales[0].bitcast(I32))
-        nc.sync.dma_start(out=words[:, 1024:T].bitcast(I32), in_=x_rows[:, 1024:T])
+        nc.sync.dma_start(out=words[:, AHEAD:T].bitcast(I32), in_=x_rows[:, AHEAD:T])
         nc.sync.dma_start(out=w_first[:], in_=w_rows[:, 0:2, :])
-        nc.sync.dma_start(out=w_raw[:], in_=w_rows[:, 2:PACK, :])
+        nc.sync.dma_start(out=w_second[:], in_=w_rows[:, 2:PACK, :])
 
-        w_bf = keep.tile([P, N, PACK], BF16, name="w_bf", align_bytes=64)
-        w_codes = keep.tile([P, N], U32, name="w_codes", align_bytes=64)
-        w_scales = keep.tile([P, N], U8, name="w_scales", align_bytes=64)
+        n_p = len(PIECES)
+        counts = keep.tile([P, n_p + 2, 3], F32, name="counts")
+        nc.vector.memset(counts[:], 0.0)
+        nc.vector.memset(counts[:, 0 : n_p + 2 : n_p + 1, 0], TINY)
+        nc.vector.memset(counts[:, n_p + 1, 1:2], 1.0 / TINY)
 
         planes = []
         for h in range(2):
@@ -59,60 +66,71 @@ def tile_picked_rank_none_p_kernel(tc, x_words, x_scales, w1, offs, out):
                 nc.sync.dma_start(out=plane[r:P:32, :].bitcast(I32), in_=picked_scales[32 + 4 * r : 96 : 16, :].bitcast(I32))
             planes.append(plane)
 
-        picked = [keep.tile([P, HALF], U32, name="picked0", tag="turns", align_bytes=64)]
-        nc.vector.tensor_copy(picked[0][:], words[:].indirect(offsets[:, 0 : HALF // 16]))
-        nc.scalar.activation(w_bf[:, :, 0:2].rearrange("p (c i) j -> p c j i", i=4), w_first[:].rearrange("p j (c i) -> p c j i", i=4), COPY)
+        picked = []
+
+        def gather(tag):
+            a = sum(GATHERS[: len(picked)])
+            b = a + GATHERS[len(picked)]
+            tile = keep.tile([P, b - a], U32, name=f"picked{len(picked)}", tag=tag, align_bytes=64)
+            nc.vector.tensor_copy(tile[:], words[:].indirect(offsets[:, a // 16 : b // 16]))
+            picked.append((a, b, tile))
+
+        gather("picked")
+
+        w_codes = keep.tile([P, N], U32, name="w_codes", align_bytes=64)
+        w_scales = keep.tile([P, N], U8, name="w_scales", align_bytes=64)
+        nc.scalar.activation(w_bf[:, :, 0:2].rearrange("p (c i) j -> p c j i", i=4), w_first[:].rearrange("p j (c i) -> p c j i", i=4), COPY, scale=-1.0)
         for a in (0, N // 2):
             b = a + N // 2
-            nc.scalar.activation(w_bf[:, a:b, 2:PACK].rearrange("p (c i) j -> p c j i", i=4), w_raw[:, :, a:b].rearrange("p j (c i) -> p c j i", i=4), COPY)
+            nc.scalar.activation(w_bf[:, a:b, 2:PACK].rearrange("p (c i) j -> p c j i", i=4), w_second[:, :, a:b].rearrange("p j (c i) -> p c j i", i=4), COPY, scale=-1.0)
             nc.vector.quantize_mx(out=w_codes[:, a:b].bitcast(FP8X4), scales=w_scales[:, a:b], in_=w_bf[:, a:b, :].rearrange("p n j -> p (n j)"))
-        picked.append(keep.tile([P, HALF], U32, name="picked1", tag="late", align_bytes=64))
-        nc.vector.tensor_copy(picked[1][:], words[:].indirect(offsets[:, HALF // 16 : S // 16]))
+        gather("after_cast")
 
-        n_p = len(PIECES)
-        neg_max = keep.tile([P, n_p], F32, name="neg_max")
-        sums = keep.tile([P, n_p], F32, name="sums")
-        exps = []
-        c0 = 0
-        for i, width in enumerate(PIECES):
-            acc = psum.tile([P, width], F32, name=f"acc{i}")
-            nc.tensor.matmul_mx(
-                out=acc[:],
-                lhsT=w_codes[:].bitcast(FP8X4),
-                lhsT_scale=w_scales[:],
-                rhs=picked[c0 // HALF][:, c0 % HALF : c0 % HALF + width].bitcast(FP8X4),
-                rhs_scale=planes[c0 // HALF][:, c0 % HALF : c0 % HALF + width],
-                start=True,
-                stop=True,
-            )
-            nc.vector.tensor_reduce(neg_max[:, i : i + 1], acc[:], AX, ALU.max, negate=True)
-            e = keep.tile([P, width], F32, name=f"e{i}")
-            nc.scalar.activation(e[:], acc[:], EXP, bias=neg_max[:, i : i + 1], accum_out=sums[:, i : i + 1])
-            exps.append((c0, width, e))
-            c0 = c0 + width
+        def product(i):
+            acc = psum.tile([P, sum(PIECES[i])], F32, name=f"acc{i}")
+            first = sum(sum(widths) for widths in PIECES[:i])
+            c = first
+            for width in PIECES[i]:
+                a, b, tile = [g for g in picked if g[0] <= c < g[1]][0]
+                nc.tensor.matmul_mx(
+                    out=acc[:, c - first : c - first + width],
+                    lhsT=w_codes[:].bitcast(FP8X4),
+                    lhsT_scale=w_scales[:],
+                    rhs=tile[:, c - a : c - a + width].bitcast(FP8X4),
+                    rhs_scale=planes[c // HALF][:, c % HALF : c % HALF + width],
+                    start=True,
+                    stop=True,
+                )
+                c = c + width
+            return acc
 
-        neg_top = keep.tile([P, 1], F32, name="neg_top")
-        nc.vector.tensor_reduce(neg_top[:], neg_max[:, 0 : n_p - 1], AX, ALU.min)
-        adjust = keep.tile([P, n_p], F32, name="adjust")
-        nc.scalar.activation(adjust[:], neg_max[:], EXP, bias=neg_top[:], scale=-1.0)
-        terms = keep.tile([P, n_p], F32, name="terms")
-        total = keep.tile([P, 1], F32, name="total")
-        nc.vector.scalar_tensor_tensor(terms[:], adjust[:], CAP, sums[:], ALU.min, ALU.mult, accum_out=total[:])
-        capped = keep.tile([P, n_p], F32, name="capped")
-        nc.vector.tensor_scalar(capped[:], adjust[:], CAP, None, ALU.min)
-        recip = keep.tile([P, 1], F32, name="recip")
-        nc.vector.reciprocal(recip[:], total[:])
+        low = keep.tile([P, n_p - 1], F32, name="low")
+        sums = keep.tile([P, n_p - 1], F32, name="sums")
+        exps = [keep.tile([P, sum(widths)], F32, name=f"e{i}") for i, widths in enumerate(PIECES)]
+        for i in range(n_p - 1):
+            if i == EARLY:
+                gather("after_second")
+            acc = product(i)
+            nc.vector.tensor_reduce(low[:, i : i + 1], acc[:], AX, ALU.min)
+            nc.scalar.activation(exps[i][:], acc[:], EXP, bias=low[:, i : i + 1], scale=-1.0, accum_out=sums[:, i : i + 1])
 
-        pre = keep.tile([P, 256], F32, name="pre")
-        for i in (2, 3):
-            p0, pw, e = exps[i]
-            nc.scalar.activation(pre[:, p0 - HALF : p0 - HALF + pw], e[:], COPY, scale=adjust[:, i : i + 1])
-        head = keep.tile([P, 256], F32, name="head")
-        rest = keep.tile([P, 768], F32, name="rest")
-        nc.vector.tensor_scalar(head[:], exps[0][2][:], capped[:, 0:1], recip[:], ALU.mult, ALU.mult)
-        nc.sync.dma_start(out=out[:, 0:256], in_=head[:])
-        nc.scalar.activation(rest[:, 256:512], pre[:], COPY, scale=recip[:])
-        for i in (1, 4, 5):
-            p0, pw, e = exps[i]
-            nc.vector.tensor_scalar(rest[:, p0 - 256 : p0 - 256 + pw], e[:], capped[:, i : i + 1], recip[:], ALU.mult, ALU.mult)
-        nc.sync.dma_start(out=out[:, 256:S], in_=rest[:])
+        acc = product(n_p - 1)
+        clipped = keep.tile([P, sum(PIECES[-1])], F32, name="clipped")
+        lowest = keep.tile([P, 1], F32, name="lowest")
+        nc.vector.tensor_scalar(clipped[:], acc[:], low[:, 0:1], low[:, 1:2], ALU.min, ALU.min, accum_out=lowest[:])
+        adjust = keep.tile([P, n_p - 1], F32, name="adjust")
+        nc.scalar.activation(adjust[:], low[:], EXP, bias=lowest[:], scale=-1.0)
+        nc.scalar.activation(exps[-1][:], acc[:], EXP, bias=lowest[:], scale=-1.0, accum_out=counts[:, n_p, 0:1])
+        nc.vector.tensor_tensor(counts[:, 1:n_p, 0], adjust[:], sums[:], ALU.mult)
+        stats = keep.tile([P, 2], F32, name="stats")
+        nc.vector.bn_aggr(stats[:], counts[:].rearrange("p a b -> p (a b)"))
+        recip = stats[:, 0:1]
+
+        head = keep.tile([P, HEAD], F32, name="head")
+        rest = keep.tile([P, S - HEAD], F32, name="rest")
+        nc.vector.tensor_scalar(head[:], exps[0][:, 0:HEAD], adjust[:, 0:1], recip, ALU.mult, ALU.mult)
+        nc.sync.dma_start(out=out[:, 0:HEAD], in_=head[:])
+        nc.scalar.activation(rest[:, 512:768], exps[2][:], COPY, scale=recip)
+        nc.vector.tensor_scalar(rest[:, 0:128], exps[0][:, HEAD:384], adjust[:, 0:1], recip, ALU.mult, ALU.mult)
+        nc.vector.tensor_scalar(rest[:, 128:512], exps[1][:], adjust[:, 1:2], recip, ALU.mult, ALU.mult)
+        nc.sync.dma_start(out=out[:, HEAD:S], in_=rest[:])

@@ -22,10 +22,11 @@ PACK = 4
 AHEAD = 1024
 HALF = S // 2
 GATHERS = [512,256,256]
-PIECES = [[256,128],[128,256],[256]]
+PIECES = [[256],[256],[256],[256]]
 EARLY = 0
 HEAD = 256
 TINY = 2.0**-40
+CAP = 2.0**60
 
 
 def tile_picked_rank_none_p_kernel(tc, x_words, x_scales, w1, offs, out):
@@ -121,16 +122,18 @@ def tile_picked_rank_none_p_kernel(tc, x_words, x_scales, w1, offs, out):
         adjust = keep.tile([P, n_p - 1], F32, name="adjust")
         nc.scalar.activation(adjust[:], low[:], EXP, bias=lowest[:], scale=-1.0)
         nc.scalar.activation(exps[-1][:], acc[:], EXP, bias=lowest[:], scale=-1.0, accum_out=counts[:, n_p, 0:1])
-        nc.vector.tensor_tensor(counts[:, 1:n_p, 0], adjust[:], sums[:], ALU.mult)
+        nc.vector.scalar_tensor_tensor(counts[:, 1:n_p, 0], adjust[:], CAP, sums[:], ALU.min, ALU.mult)
+        capped = keep.tile([P, 1], F32, name="capped")
+        nc.vector.tensor_scalar(capped[:], adjust[:, 2:3], CAP, None, ALU.min)
         stats = keep.tile([P, 2], F32, name="stats")
         nc.vector.bn_aggr(stats[:], counts[:].rearrange("p a b -> p (a b)"))
         recip = stats[:, 0:1]
 
         head = keep.tile([P, HEAD], F32, name="head")
         rest = keep.tile([P, S - HEAD], F32, name="rest")
-        nc.vector.tensor_scalar(head[:], exps[0][:, 0:HEAD], adjust[:, 0:1], recip, ALU.mult, ALU.mult)
+        nc.vector.tensor_scalar(head[:], exps[0][:], adjust[:, 0:1], recip, ALU.mult, ALU.mult)
         nc.sync.dma_start(out=out[:, 0:HEAD], in_=head[:])
-        nc.scalar.activation(rest[:, 512:768], exps[2][:], COPY, scale=recip)
-        nc.vector.tensor_scalar(rest[:, 0:128], exps[0][:, HEAD:384], adjust[:, 0:1], recip, ALU.mult, ALU.mult)
-        nc.vector.tensor_scalar(rest[:, 128:512], exps[1][:], adjust[:, 1:2], recip, ALU.mult, ALU.mult)
+        nc.scalar.activation(rest[:, 512:768], exps[3][:], COPY, scale=recip)
+        nc.vector.tensor_scalar(rest[:, 0:256], exps[1][:], adjust[:, 1:2], recip, ALU.mult, ALU.mult)
+        nc.vector.tensor_scalar(rest[:, 256:512], exps[2][:], capped[:], recip, ALU.mult, ALU.mult)
         nc.sync.dma_start(out=out[:, HEAD:S], in_=rest[:])

@@ -58,13 +58,13 @@ def tile_picked_rank_none_p_kernel(tc, x_words, x_scales, w1, offs, out):
         nc.vector.memset(counts[:, 0 : n_p + 2 : n_p + 1, 0], TINY)
         nc.vector.memset(counts[:, n_p + 1, 1:2], 1.0 / TINY)
 
+        picked_scales = keep.tile([P, S], U8, name="picked_scales", align_bytes=64)
+        nc.vector.tensor_copy(picked_scales[:], scales[:].indirect(offsets[:]))
         planes = []
-        for h in range(2):
-            picked_scales = keep.tile([P, HALF], U8, name=f"picked_scales{h}", align_bytes=64)
-            nc.vector.tensor_copy(picked_scales[:], scales[:].indirect(offsets[:, h * HALF // 16 : (h + 1) * HALF // 16]))
-            plane = keep.tile([P, HALF], U8, name=f"plane{h}", align_bytes=64)
+        for a, b in ((0, S - GATHERS[-1]), (S - GATHERS[-1], S)):
+            plane = keep.tile([P, b - a], U8, name=f"plane{len(planes)}", align_bytes=64)
             for r in range(4):
-                nc.sync.dma_start(out=plane[r:P:32, :].bitcast(I32), in_=picked_scales[32 + 4 * r : 96 : 16, :].bitcast(I32))
+                nc.sync.dma_start(out=plane[r:P:32, :].bitcast(I32), in_=picked_scales[32 + 4 * r : 96 : 16, a:b].bitcast(I32))
             planes.append(plane)
 
         picked = []
@@ -98,7 +98,7 @@ def tile_picked_rank_none_p_kernel(tc, x_words, x_scales, w1, offs, out):
                     lhsT=w_codes[:].bitcast(FP8X4),
                     lhsT_scale=w_scales[:],
                     rhs=tile[:, c - a : c - a + width].bitcast(FP8X4),
-                    rhs_scale=planes[c // HALF][:, c % HALF : c % HALF + width],
+                    rhs_scale=planes[c // 768][:, c % 768 : c % 768 + width],
                     start=True,
                     stop=True,
                 )

@@ -81,9 +81,12 @@ def tile_picked_rank_none_p_kernel(tc, x_words, x_scales, w1, offs, out):
         w_codes = keep.tile([P, N], U32, name="w_codes", align_bytes=64)
         w_scales = keep.tile([P, N], U8, name="w_scales", align_bytes=64)
         nc.scalar.activation(w_bf[:, :, 0:2].rearrange("p (c i) j -> p c j i", i=4), w_first[:].rearrange("p j (c i) -> p c j i", i=4), COPY, scale=-1.0)
+        dst = w_bf[:, :, 2:PACK].rearrange("p (c i) j -> p c j i", i=4)
+        src = w_second[:].rearrange("p j (c i) -> p c j i", i=4)
+        nc.scalar.activation(dst[:, 0:16], src[:, 0:16], COPY, scale=-1.0)
+        nc.gpsimd.tensor_scalar(dst[:, 16:32], src[:, 16:32], -1.0, 0.0, ALU.mult, ALU.add)
         for a in (0, N // 2):
             b = a + N // 2
-            nc.scalar.activation(w_bf[:, a:b, 2:PACK].rearrange("p (c i) j -> p c j i", i=4), w_second[:, :, a:b].rearrange("p j (c i) -> p c j i", i=4), COPY, scale=-1.0)
             nc.vector.quantize_mx(out=w_codes[:, a:b].bitcast(FP8X4), scales=w_scales[:, a:b], in_=w_bf[:, a:b, :].rearrange("p n j -> p (n j)"))
         gather("after_cast")
 

@@ -20,10 +20,10 @@ AX = mybir.AxisListType.X
 P = 128
 PACK = 4
 AHEAD = 1024
-HALF = S // 2
-GATHERS = [512,256,256]
-PIECES = [[256],[256],[256],[256]]
-EARLY = 0
+EARLY = 640
+PIECE = 256
+PLANE = 768
+CAST = 80
 HEAD = 256
 TINY = 2.0**-40
 CAP = 2.0**60
@@ -38,94 +38,82 @@ def tile_picked_rank_none_p_kernel(tc, x_words, x_scales, w1, offs, out):
         offsets = keep.tile([P, S // 16], U16, name="offsets")
         words = keep.tile([P, T], U32, name="words", align_bytes=64)
         scales = keep.tile([P, T], U8, name="scales", align_bytes=64)
-        w_first = keep.tile([P, 2, N], F32, name="w_first")
-        w_bf = keep.tile([P, N, PACK], BF16, name="w_bf", tag="after_second", align_bytes=64)
-        w_second = keep.tile([P, 2, N], F32, name="w_second", tag="after_cast", align_bytes=64)
+        w_raw = keep.tile([P, PACK, N], F32, name="w_raw", tag="after_cast", align_bytes=64)
+        w_bf = keep.tile([P, N, PACK], BF16, name="w_bf", align_bytes=64)
 
         nc.vector.memset(scales[:].bitcast(I32), 0)
         x_rows = x_words[0].rearrange("p n t -> p (n t)").bitcast(I32)
-        w_rows = w1.rearrange("(p j) n -> p j n", j=PACK)
         nc.sync.dma_start(out=words[:, 0:AHEAD].bitcast(I32), in_=x_rows[:, 0:AHEAD])
         nc.sync.dma_start(offsets[:], offs)
         nc.sync.dma_start(out=scales[32:96:4, :].bitcast(I32), in_=x_scales[0].bitcast(I32))
         nc.sync.dma_start(out=words[:, AHEAD:T].bitcast(I32), in_=x_rows[:, AHEAD:T])
-        nc.sync.dma_start(out=w_first[:], in_=w_rows[:, 0:2, :])
-        nc.sync.dma_start(out=w_second[:], in_=w_rows[:, 2:PACK, :])
+        nc.sync.dma_start(out=w_raw[:], in_=w1.rearrange("(p j) n -> p j n", j=PACK))
 
-        n_p = len(PIECES)
-        counts = keep.tile([P, n_p + 2, 3], F32, name="counts")
+        counts = keep.tile([P, 3, 3], F32, name="counts")
+        adjust = keep.tile([P, 4], F32, name="adjust")
+        sums = keep.tile([P, 4], F32, name="sums")
         nc.vector.memset(counts[:], 0.0)
-        nc.vector.memset(counts[:, 0 : n_p + 2 : n_p + 1, 0], TINY)
-        nc.vector.memset(counts[:, n_p + 1, 1:2], 1.0 / TINY)
+        nc.vector.memset(counts[:, 2, 0:1], TINY)
+        nc.vector.memset(counts[:, 2, 1:2], 1.0 / TINY)
+        nc.vector.memset(adjust[:, 3:4], 1.0)
+        nc.vector.memset(sums[:, 3:4], TINY)
 
         picked_scales = keep.tile([P, S], U8, name="picked_scales", align_bytes=64)
         nc.vector.tensor_copy(picked_scales[:], scales[:].indirect(offsets[:]))
         planes = []
-        for a, b in ((0, S - GATHERS[-1]), (S - GATHERS[-1], S)):
-            plane = keep.tile([P, b - a], U8, name=f"plane{len(planes)}", align_bytes=64)
+        for a, b in ((0, PLANE), (PLANE, S)):
+            plane = keep.tile([P, b - a], U8, name=f"plane{a}", align_bytes=64)
             for r in range(4):
                 nc.sync.dma_start(out=plane[r:P:32, :].bitcast(I32), in_=picked_scales[32 + 4 * r : 96 : 16, a:b].bitcast(I32))
             planes.append(plane)
 
-        picked = []
-
-        def gather(tag):
-            a = sum(GATHERS[: len(picked)])
-            b = a + GATHERS[len(picked)]
-            tile = keep.tile([P, b - a], U32, name=f"picked{len(picked)}", tag=tag, align_bytes=64)
-            nc.vector.tensor_copy(tile[:], words[:].indirect(offsets[:, a // 16 : b // 16]))
-            picked.append((a, b, tile))
-
-        gather("picked")
+        early = keep.tile([P, EARLY], U32, name="early", align_bytes=64)
+        nc.vector.tensor_copy(early[:], words[:].indirect(offsets[:, 0 : EARLY // 16]))
 
         w_codes = keep.tile([P, N], U32, name="w_codes", align_bytes=64)
         w_scales = keep.tile([P, N], U8, name="w_scales", align_bytes=64)
-        nc.scalar.activation(w_bf[:, :, 0:2].rearrange("p (c i) j -> p c j i", i=4), w_first[:].rearrange("p j (c i) -> p c j i", i=4), COPY, scale=-1.0)
-        dst = w_bf[:, :, 2:PACK].rearrange("p (c i) j -> p c j i", i=4)
-        src = w_second[:].rearrange("p j (c i) -> p c j i", i=4)
-        nc.scalar.activation(dst[:, 0:16], src[:, 0:16], COPY, scale=-1.0)
-        nc.gpsimd.tensor_scalar(dst[:, 16:32], src[:, 16:32], -1.0, 0.0, ALU.mult, ALU.add)
-        for a in (0, N // 2):
-            b = a + N // 2
-            nc.vector.quantize_mx(out=w_codes[:, a:b].bitcast(FP8X4), scales=w_scales[:, a:b], in_=w_bf[:, a:b, :].rearrange("p n j -> p (n j)"))
-        gather("after_cast")
+        dst = w_bf[:].rearrange("p (c i) j -> p c j i", i=4)
+        src = w_raw[:].rearrange("p j (c i) -> p c j i", i=4)
+        nc.scalar.activation(dst[:, 0 : CAST // 4], src[:, 0 : CAST // 4], COPY, scale=-1.0)
+        nc.gpsimd.tensor_scalar(dst[:, CAST // 4 :], src[:, CAST // 4 :], -1.0, 0.0, ALU.mult, ALU.add)
+        nc.vector.quantize_mx(out=w_codes[:].bitcast(FP8X4), scales=w_scales[:], in_=w_bf[:].rearrange("p n j -> p (n j)"))
+
+        late = keep.tile([P, S - EARLY], U32, name="late", tag="after_cast", align_bytes=64)
+        nc.vector.tensor_copy(late[:], words[:].indirect(offsets[:, EARLY // 16 :]))
 
         def product(i):
-            acc = psum.tile([P, sum(PIECES[i])], F32, name=f"acc{i}")
-            first = sum(sum(widths) for widths in PIECES[:i])
-            c = first
-            for width in PIECES[i]:
-                a, b, tile = [g for g in picked if g[0] <= c < g[1]][0]
+            acc = psum.tile([P, PIECE], F32, name=f"acc{i}")
+            first, last = i * PIECE, (i + 1) * PIECE
+            cuts = [first, EARLY, last] if first < EARLY < last else [first, last]
+            for a, b in zip(cuts[:-1], cuts[1:]):
+                codes = early[:, a:b] if a < EARLY else late[:, a - EARLY : b - EARLY]
+                plane = planes[0][:, a:b] if a < PLANE else planes[1][:, a - PLANE : b - PLANE]
                 nc.tensor.matmul_mx(
-                    out=acc[:, c - first : c - first + width],
+                    out=acc[:, a - first : b - first],
                     lhsT=w_codes[:].bitcast(FP8X4),
                     lhsT_scale=w_scales[:],
-                    rhs=tile[:, c - a : c - a + width].bitcast(FP8X4),
-                    rhs_scale=planes[c // 768][:, c % 768 : c % 768 + width],
+                    rhs=codes.bitcast(FP8X4),
+                    rhs_scale=plane,
                     start=True,
                     stop=True,
                 )
-                c = c + width
             return acc
 
-        low = keep.tile([P, n_p - 1], F32, name="low")
-        sums = keep.tile([P, n_p - 1], F32, name="sums")
-        exps = [keep.tile([P, sum(widths)], F32, name=f"e{i}") for i, widths in enumerate(PIECES)]
-        for i in range(n_p - 1):
-            if i == EARLY:
-                gather("after_second")
+        low = keep.tile([P, 3], F32, name="low")
+        exps = [keep.tile([P, PIECE], F32, name=f"e{i}") for i in range(4)]
+        for i in range(3):
             acc = product(i)
             nc.vector.tensor_reduce(low[:, i : i + 1], acc[:], AX, ALU.min)
             nc.scalar.activation(exps[i][:], acc[:], EXP, bias=low[:, i : i + 1], scale=-1.0, accum_out=sums[:, i : i + 1])
 
-        acc = product(n_p - 1)
-        clipped = keep.tile([P, sum(PIECES[-1])], F32, name="clipped")
+        acc = product(3)
+        clipped = keep.tile([P, PIECE], F32, name="clipped")
         lowest = keep.tile([P, 1], F32, name="lowest")
         nc.vector.tensor_scalar(clipped[:], acc[:], low[:, 0:1], low[:, 1:2], ALU.min, ALU.min, accum_out=lowest[:])
-        adjust = keep.tile([P, n_p - 1], F32, name="adjust")
-        nc.scalar.activation(adjust[:], low[:], EXP, bias=lowest[:], scale=-1.0)
-        nc.scalar.activation(exps[-1][:], acc[:], EXP, bias=lowest[:], scale=-1.0, accum_out=counts[:, n_p, 0:1])
-        nc.vector.scalar_tensor_tensor(counts[:, 1:n_p, 0], adjust[:], CAP, sums[:], ALU.min, ALU.mult)
+        nc.scalar.activation(adjust[:, 0:3], low[:], EXP, bias=lowest[:], scale=-1.0)
+        nc.scalar.activation(exps[3][:], acc[:], EXP, bias=lowest[:], scale=-1.0, accum_out=counts[:, 1, 0:1])
+        weighted = keep.tile([P, 4], F32, name="weighted")
+        nc.vector.scalar_tensor_tensor(weighted[:], adjust[:], CAP, sums[:], ALU.min, ALU.mult, accum_out=counts[:, 0, 0:1])
         capped = keep.tile([P, 1], F32, name="capped")
         nc.vector.tensor_scalar(capped[:], adjust[:, 2:3], CAP, None, ALU.min)
         stats = keep.tile([P, 2], F32, name="stats")

@@ -20,7 +20,8 @@ AX = mybir.AxisListType.X
 P = 128
 PACK = 4
 AHEAD = 1024
-EARLY = 640
+EARLY = 512
+LAST = 768
 PIECE = 256
 PLANE = 768
 CAST = 80
@@ -39,7 +40,7 @@ def tile_picked_rank_none_p_kernel(tc, x_words, x_scales, w1, offs, out):
         words = keep.tile([P, T], U32, name="words", align_bytes=64)
         scales = keep.tile([P, T], U8, name="scales", align_bytes=64)
         w_raw = keep.tile([P, PACK, N], F32, name="w_raw", tag="after_cast", align_bytes=64)
-        w_bf = keep.tile([P, N, PACK], BF16, name="w_bf", align_bytes=64)
+        w_bf = keep.tile([P, N, PACK], BF16, name="w_bf", tag="after_quantize", align_bytes=64)
 
         nc.vector.memset(scales[:].bitcast(I32), 0)
         x_rows = x_words[0].rearrange("p n t -> p (n t)").bitcast(I32)
@@ -78,15 +79,17 @@ def tile_picked_rank_none_p_kernel(tc, x_words, x_scales, w1, offs, out):
         nc.gpsimd.tensor_scalar(dst[:, CAST // 4 :], src[:, CAST // 4 :], -1.0, 0.0, ALU.mult, ALU.add)
         nc.vector.quantize_mx(out=w_codes[:].bitcast(FP8X4), scales=w_scales[:], in_=w_bf[:].rearrange("p n j -> p (n j)"))
 
-        late = keep.tile([P, S - EARLY], U32, name="late", tag="after_cast", align_bytes=64)
-        nc.vector.tensor_copy(late[:], words[:].indirect(offsets[:, EARLY // 16 :]))
+        late = keep.tile([P, LAST - EARLY], U32, name="late", tag="after_cast", align_bytes=64)
+        nc.vector.tensor_copy(late[:], words[:].indirect(offsets[:, EARLY // 16 : LAST // 16]))
+        final = keep.tile([P, S - LAST], U32, name="final", tag="after_quantize", align_bytes=64)
+        nc.vector.tensor_copy(final[:], words[:].indirect(offsets[:, LAST // 16 :]))
 
         def product(i):
             acc = psum.tile([P, PIECE], F32, name=f"acc{i}")
             first, last = i * PIECE, (i + 1) * PIECE
             cuts = [first, EARLY, last] if first < EARLY < last else [first, last]
             for a, b in zip(cuts[:-1], cuts[1:]):
-                codes = early[:, a:b] if a < EARLY else late[:, a - EARLY : b - EARLY]
+                codes = early[:, a:b] if a < EARLY else late[:] if a < LAST else final[:]
                 plane = planes[0][:, a:b] if a < PLANE else planes[1][:, a - PLANE : b - PLANE]
                 nc.tensor.matmul_mx(
                     out=acc[:, a - first : b - first],

@@ -75,9 +75,12 @@ def tile_picked_rank_none_p_kernel(tc, x_words, x_scales, w1, offs, out):
         w_scales = keep.tile([P, N], U8, name="w_scales", align_bytes=64)
         dst = w_bf[:].rearrange("p (c i) j -> p c j i", i=4)
         src = w_raw[:].rearrange("p j (c i) -> p c j i", i=4)
-        nc.scalar.activation(dst[:, 0 : CAST // 4], src[:, 0 : CAST // 4], COPY, scale=-1.0)
+        for a, b in ((0, N // 2), (N // 2, CAST)):
+            nc.scalar.activation(dst[:, a // 4 : b // 4], src[:, a // 4 : b // 4], COPY, scale=-1.0)
         nc.gpsimd.tensor_scalar(dst[:, CAST // 4 :], src[:, CAST // 4 :], -1.0, 0.0, ALU.mult, ALU.add)
-        nc.vector.quantize_mx(out=w_codes[:].bitcast(FP8X4), scales=w_scales[:], in_=w_bf[:].rearrange("p n j -> p (n j)"))
+        for a in (0, N // 2):
+            b = a + N // 2
+            nc.vector.quantize_mx(out=w_codes[:, a:b].bitcast(FP8X4), scales=w_scales[:, a:b], in_=w_bf[:, a:b, :].rearrange("p n j -> p (n j)"))
 
         late = keep.tile([P, LAST - EARLY], U32, name="late", tag="after_cast", align_bytes=64)
         nc.vector.tensor_copy(late[:], words[:].indirect(offsets[:, EARLY // 16 : LAST // 16]))

@@ -107,15 +107,18 @@ def tile_picked_rank_none_p_kernel(tc, x_words, x_scales, w1, offs, out):
 
         low = keep.tile([P, 3], F32, name="low")
         exps = [keep.tile([P, PIECE], F32, name=f"e{i}") for i in range(4)]
+        pair = keep.tile([P, 2], F32, name="pair")
         for i in range(3):
             acc = product(i)
-            nc.vector.tensor_reduce(low[:, i : i + 1], acc[:], AX, ALU.min)
-            nc.scalar.activation(exps[i][:], acc[:], EXP, bias=low[:, i : i + 1], scale=-1.0, accum_out=sums[:, i : i + 1])
+            own = pair[:, i : i + 1] if i < 2 else low[:, 2:3]
+            nc.vector.tensor_reduce(own, acc[:], AX, ALU.min)
+            nc.scalar.activation(exps[i][:], acc[:], EXP, bias=own, scale=-1.0, accum_out=sums[:, i : i + 1])
+        nc.vector.tensor_copy(low[:, 0:2], pair[:])
 
         acc = product(3)
         clipped = keep.tile([P, PIECE], F32, name="clipped")
         lowest = keep.tile([P, 1], F32, name="lowest")
-        nc.vector.tensor_scalar(clipped[:], acc[:], low[:, 0:1], low[:, 1:2], ALU.min, ALU.min, accum_out=lowest[:])
+        nc.vector.tensor_scalar(clipped[:], acc[:], pair[:, 0:1], pair[:, 1:2], ALU.min, ALU.min, accum_out=lowest[:])
         nc.scalar.activation(adjust[:, 0:3], low[:], EXP, bias=lowest[:], scale=-1.0)
         nc.scalar.activation(exps[3][:], acc[:], EXP, bias=lowest[:], scale=-1.0, accum_out=counts[:, 1, 0:1])
         weighted = keep.tile([P, 4], F32, name="weighted")

@@ -117,13 +117,13 @@ def tile_picked_rank_none_p_kernel(tc, x_words, x_scales, w1, offs, out):
 
         acc = product(3)
         clipped = keep.tile([P, PIECE], F32, name="clipped")
-        lowest = keep.tile([P, 1], F32, name="lowest")
+        lowest = keep.tile([P, 1], F32, name="lowest", tag="after_last_exp")
         nc.vector.tensor_scalar(clipped[:], acc[:], pair[:, 0:1], pair[:, 1:2], ALU.min, ALU.min, accum_out=lowest[:])
         nc.scalar.activation(adjust[:, 0:3], low[:], EXP, bias=lowest[:], scale=-1.0)
         nc.scalar.activation(exps[3][:], acc[:], EXP, bias=lowest[:], scale=-1.0, accum_out=counts[:, 1, 0:1])
         weighted = keep.tile([P, 4], F32, name="weighted")
         nc.vector.scalar_tensor_tensor(weighted[:], adjust[:], CAP, sums[:], ALU.min, ALU.mult, accum_out=counts[:, 0, 0:1])
-        capped = keep.tile([P, 1], F32, name="capped")
+        capped = keep.tile([P, 1], F32, name="capped", tag="after_last_exp")
         nc.vector.tensor_scalar(capped[:], adjust[:, 2:3], CAP, None, ALU.min)
         stats = keep.tile([P, 2], F32, name="stats")
         nc.vector.bn_aggr(stats[:], counts[:].rearrange("p a b -> p (a b)"))

@@ -24,7 +24,7 @@ EARLY = 512
 LAST = 768
 PIECE = 256
 PLANE = 768
-CAST = 80
+CAST = 96
 HEAD = 256
 TINY = 2.0**-40
 CAP = 2.0**60
@@ -77,9 +77,8 @@ def tile_picked_rank_none_p_kernel(tc, x_words, x_scales, w1, offs, out):
         src = w_raw[:].rearrange("p j (c i) -> p c j i", i=4)
         for a, b in ((0, N // 2), (N // 2, CAST)):
             nc.scalar.activation(dst[:, a // 4 : b // 4], src[:, a // 4 : b // 4], COPY, scale=-1.0)
-        nc.gpsimd.tensor_scalar(dst[:, CAST // 4 :], src[:, CAST // 4 :], -1.0, 0.0, ALU.mult, ALU.add)
-        for a in (0, N // 2):
-            b = a + N // 2
+        nc.gpsimd.tensor_scalar(w_bf[:, CAST:, :], w_raw[:, :, CAST:].rearrange("p j n -> p n j"), -1.0, 0.0, ALU.mult, ALU.add)
+        for a, b in ((0, 64), (96, N), (64, 96)):
             nc.vector.quantize_mx(out=w_codes[:, a:b].bitcast(FP8X4), scales=w_scales[:, a:b], in_=w_bf[:, a:b, :].rearrange("p n j -> p (n j)"))
 
         late = keep.tile([P, LAST - EARLY], U32, name="late", tag="after_cast", align_bytes=64)

from contextlib import ExitStack

import concourse.mybir as mybir

K, T, S, N = 512, 4096, 1024, 128
FLOPS = 2 * K * S * N

F32 = mybir.dt.float32
BF16 = mybir.dt.bfloat16
I32 = mybir.dt.int32
U32 = mybir.dt.uint32
U16 = mybir.dt.uint16
U8 = mybir.dt.uint8
FP8X4 = mybir.dt.float8_e4m3fn_x4
ALU = mybir.AluOpType
EXP = mybir.ActivationFunctionType.Exp
COPY = mybir.ActivationFunctionType.Copy
AX = mybir.AxisListType.X

P = 128
PACK = 4
AHEAD = 1024
EARLY = 512
LAST = 768
PIECE = 256
PLANE = 768
CAST = 96
HEAD = 256
TINY = 2.0**-40
CAP = 2.0**60


def tile_picked_rank_none_p_kernel(tc, x_words, x_scales, w1, offs, out):
    nc = tc.nc
    with ExitStack() as ctx:
        keep = ctx.enter_context(tc.tile_pool(name="keep", bufs=1))
        psum = ctx.enter_context(tc.psum_pool(name="psum", bufs=1))

        offsets = keep.tile([P, S // 16], U16, name="offsets")
        words = keep.tile([P, T], U32, name="words", align_bytes=64)
        scales = keep.tile([P, T], U8, name="scales", align_bytes=64)
        w_raw = keep.tile([P, PACK, N], F32, name="w_raw", tag="after_cast", align_bytes=64)
        w_bf = keep.tile([P, N, PACK], BF16, name="w_bf", tag="after_quantize", align_bytes=64)

        nc.vector.memset(scales[:].bitcast(I32), 0)
        x_rows = x_words[0].rearrange("p n t -> p (n t)").bitcast(I32)
        nc.sync.dma_start(out=words[:, 0:AHEAD].bitcast(I32), in_=x_rows[:, 0:AHEAD])
        nc.sync.dma_start(offsets[:], offs)
        nc.sync.dma_start(out=scales[32:96:4, :].bitcast(I32), in_=x_scales[0].bitcast(I32))
        nc.sync.dma_start(out=words[:, AHEAD:T].bitcast(I32), in_=x_rows[:, AHEAD:T])
        nc.sync.dma_start(out=w_raw[:], in_=w1.rearrange("(p j) n -> p j n", j=PACK))

        counts = keep.tile([P, 3, 3], F32, name="counts")
        adjust = keep.tile([P, 4], F32, name="adjust")
        sums = keep.tile([P, 4], F32, name="sums")
        nc.vector.memset(counts[:], 0.0)
        nc.vector.memset(counts[:, 2, 0:1], TINY)
        nc.vector.memset(counts[:, 2, 1:2], 1.0 / TINY)
        nc.vector.memset(adjust[:, 3:4], 1.0)
        nc.vector.memset(sums[:, 3:4], TINY)

        picked_scales = keep.tile([P, S], U8, name="picked_scales", align_bytes=64)
        nc.vector.tensor_copy(picked_scales[:], scales[:].indirect(offsets[:]))
        planes = []
        for a, b in ((0, PLANE), (PLANE, S)):
            plane = keep.tile([P, b - a], U8, name=f"plane{a}", align_bytes=64)
            for r in range(4):
                nc.sync.dma_start(out=plane[r:P:32, :].bitcast(I32), in_=picked_scales[32 + 4 * r : 96 : 16, a:b].bitcast(I32))
            planes.append(plane)

        early = keep.tile([P, EARLY], U32, name="early", align_bytes=64)
        nc.vector.tensor_copy(early[:], words[:].indirect(offsets[:, 0 : EARLY // 16]))

        w_codes = keep.tile([P, N], U32, name="w_codes", align_bytes=64)
        w_scales = keep.tile([P, N], U8, name="w_scales", align_bytes=64)
        dst = w_bf[:].rearrange("p (c i) j -> p c j i", i=4)
        src = w_raw[:].rearrange("p j (c i) -> p c j i", i=4)
        for a, b in ((0, N // 2), (N // 2, CAST)):
            nc.scalar.activation(dst[:, a // 4 : b // 4], src[:, a // 4 : b // 4], COPY, scale=-1.0)
        nc.gpsimd.tensor_scalar(w_bf[:, CAST:, :], w_raw[:, :, CAST:].rearrange("p j n -> p n j"), -1.0, 0.0, ALU.mult, ALU.add)
        for a, b in ((0, 64), (96, N), (64, 96)):
            nc.vector.quantize_mx(out=w_codes[:, a:b].bitcast(FP8X4), scales=w_scales[:, a:b], in_=w_bf[:, a:b, :].rearrange("p n j -> p (n j)"))

        late = keep.tile([P, LAST - EARLY], U32, name="late", tag="after_cast", align_bytes=64)
        nc.vector.tensor_copy(late[:], words[:].indirect(offsets[:, EARLY // 16 : LAST // 16]))
        final = keep.tile([P, S - LAST], U32, name="final", tag="after_quantize", align_bytes=64)
        nc.vector.tensor_copy(final[:], words[:].indirect(offsets[:, LAST // 16 :]))

        def product(i):
            acc = psum.tile([P, PIECE], F32, name=f"acc{i}")
            first, last = i * PIECE, (i + 1) * PIECE
            cuts = [first, EARLY, last] if first < EARLY < last else [first, last]
            for a, b in zip(cuts[:-1], cuts[1:]):
                codes = early[:, a:b] if a < EARLY else late[:] if a < LAST else final[:]
                plane = planes[0][:, a:b] if a < PLANE else planes[1][:, a - PLANE : b - PLANE]
                nc.tensor.matmul_mx(
                    out=acc[:, a - first : b - first],
                    lhsT=w_codes[:].bitcast(FP8X4),
                    lhsT_scale=w_scales[:],
                    rhs=codes.bitcast(FP8X4),
                    rhs_scale=plane,
                    start=True,
                    stop=True,
                )
            return acc

        low = keep.tile([P, 3], F32, name="low")
        exps = [keep.tile([P, PIECE], F32, name=f"e{i}") for i in range(4)]
        pair = keep.tile([P, 2], F32, name="pair")
        for i in range(3):
            acc = product(i)
            own = pair[:, i : i + 1] if i < 2 else low[:, 2:3]
            nc.vector.tensor_reduce(own, acc[:], AX, ALU.min)
            nc.scalar.activation(exps[i][:], acc[:], EXP, bias=own, scale=-1.0, accum_out=sums[:, i : i + 1])
        nc.vector.tensor_copy(low[:, 0:2], pair[:])

        acc = product(3)
        clipped = keep.tile([P, PIECE], F32, name="clipped")
        lowest = keep.tile([P, 1], F32, name="lowest", tag="after_last_exp")
        nc.vector.tensor_scalar(clipped[:], acc[:], pair[:, 0:1], pair[:, 1:2], ALU.min, ALU.min, accum_out=lowest[:])
        nc.scalar.activation(adjust[:, 0:3], low[:], EXP, bias=lowest[:], scale=-1.0)
        nc.scalar.activation(exps[3][:], acc[:], EXP, bias=lowest[:], scale=-1.0, accum_out=counts[:, 1, 0:1])
        weighted = keep.tile([P, 4], F32, name="weighted")
        nc.vector.scalar_tensor_tensor(weighted[:], adjust[:], CAP, sums[:], ALU.min, ALU.mult, accum_out=counts[:, 0, 0:1])
        capped = keep.tile([P, 1], F32, name="capped", tag="after_last_exp")
        nc.vector.tensor_scalar(capped[:], adjust[:, 2:3], CAP, None, ALU.min)
        stats = keep.tile([P, 2], F32, name="stats")
        nc.vector.bn_aggr(stats[:], counts[:].rearrange("p a b -> p (a b)"))
        recip = stats[:, 0:1]

        head = keep.tile([P, HEAD], F32, name="head")
        rest = keep.tile([P, S - HEAD], F32, name="rest")
        nc.vector.tensor_scalar(head[:], exps[0][:], adjust[:, 0:1], recip, ALU.mult, ALU.mult)
        nc.sync.dma_start(out=out[:, 0:HEAD], in_=head[:])
        nc.scalar.activation(rest[:, 512:768], exps[3][:], COPY, scale=recip)
        nc.vector.tensor_scalar(rest[:, 0:256], exps[1][:], adjust[:, 1:2], recip, ALU.mult, ALU.mult)
        nc.vector.tensor_scalar(rest[:, 256:512], exps[2][:], capped[:], recip, ALU.mult, ALU.mult)
        nc.sync.dma_start(out=out[:, HEAD:S], in_=rest[:])
